import numpy as np
import ml_dtypes


def mxq(x, axis, fmt="e4m3"):
    dtype, down = {"e4m3": (ml_dtypes.float8_e4m3fn, 7), "e5m2": (ml_dtypes.float8_e5m2, 14)}[fmt]
    v = np.moveaxis(np.asarray(x, np.float32).astype(ml_dtypes.bfloat16).astype(np.float64), axis, -1)
    blocks = v.reshape(v.shape[:-1] + (-1, 32))
    amax = np.abs(blocks).max(-1, keepdims=True)
    byte = np.maximum(np.where(amax > 0, np.frexp(amax)[1] - 1 + 127, 0) - down, 1)
    scale = np.exp2(byte - 127.0)
    codes = (blocks / scale).astype(np.float32).astype(dtype).astype(np.float64)
    return np.moveaxis((codes * scale).reshape(v.shape), -1, axis)


WIDE = False


def mx_kscale(k):
    if not WIDE:
        return np.ones(k)
    levels = np.array([10, -10, 5, -5, 0])
    if k % 512:
        return np.exp2(np.random.permutation(np.resize(levels, k // 32))).repeat(32)
    a = np.empty((k // 512, 16))
    for p in range(k // 512):
        a[p, :8] = np.random.permutation(np.resize(levels, 8))
        for g in range(8):
            far = levels[np.abs(levels - a[p, g]) >= 10]
            a[p, g + 8] = far[np.random.randint(len(far))]
    return np.exp2(a.ravel()).repeat(32)


def f64(x):
    return np.asarray(x).astype(np.float64)


def striped(idx):
    return np.tile(idx.reshape(-1, 16).T, (8, 1)).astype(np.uint16)


def unstriped(offs):
    return offs[:16].T.reshape(-1).astype(np.int64)


def striped8(idx):
    return np.concatenate([x.reshape(-1, 16).T for x in idx]).astype(np.uint16)


def runs(offs, k):
    lists = np.stack([offs[16 * r : 16 * r + 16].T.reshape(-1) for r in range(8)]).astype(np.int64)
    return lists[np.arange(k) % 512 // 64]


def pack_weight(w):
    k, n = w.shape
    w = f64(np.asarray(w, np.float32).astype(ml_dtypes.bfloat16)).reshape(k // 32, 32, n)
    amax = np.abs(w).max(1)
    byte = np.clip(np.where(amax > 0, np.frexp(amax)[1] - 1 + 127 - 7, 1), 1, 254)
    scaled = (w * np.exp2(127.0 - byte)[:, None, :]).reshape(k, n).astype(np.float32)
    words = np.ascontiguousarray(scaled.reshape(k // 512, 128, 4, n).transpose(0, 1, 3, 2)).astype(ml_dtypes.float8_e4m3fn).view(np.uint8)
    return words, np.ascontiguousarray(byte.astype(np.uint8).reshape(k // 512, 16, n))


def unpack_weight(words, scales):
    g, p, n, _ = words.shape
    vals = np.ascontiguousarray(words).view(ml_dtypes.float8_e4m3fn).astype(np.float64) * np.repeat(np.exp2(scales.astype(np.float64) - 127.0), 8, axis=1)[..., None]
    return vals.transpose(0, 1, 3, 2).reshape(g * 512, n)


def sigmoid(v):
    return 1.0 / (1.0 + np.exp(-np.maximum(v, -700.0)))


K, T, S, N, G, H, W = 512, 1024, 256, 512, 2048, 512, 1024


def setup_inputs():
    n = np.random.standard_normal
    s = mx_kscale(K)[:, None]
    u = mx_kscale(K)
    packed_xT = pack_weight(n((K, T)) * s)
    packed_dT = pack_weight(n((K, G)) / s)
    return {
        "x_words": packed_xT[0],
        "x_scales": packed_xT[1],
        "d_words": packed_dT[0],
        "d_scales": packed_dT[1],
        "gn": (np.random.uniform(0.5, 1.5, (H, 1)) * u[:, None]).astype(np.float32),
        "gm": (np.random.uniform(0.5, 1.5, (H, 1)) * u[:, None]).astype(np.float32),
        "w1": (n((H, N)) / np.sqrt(2 * H) / u[:, None]).astype(np.float32),
        "w2": (n((H, N)) / np.sqrt(2 * H) / u[:, None]).astype(np.float32),
        "offs": striped(np.random.permutation(T)[:S]),
        "k1": striped8(np.random.randint(0, G, (8, H))),
        "two": striped(np.random.permutation(T)[:S]),
        "n1": striped(np.random.randint(0, S, W)),
        "n2": striped8(np.stack([np.random.permutation(S) for _ in range(8)])),
        "n3": striped8(np.stack([np.random.permutation(S) for _ in range(8)])),
        "n4": striped(np.random.permutation(S)),
        "n5": striped(np.random.permutation(S)),
    }


def reference(x_words, x_scales, d_words, d_scales, gn, gm, w1, w2, offs, k1, two, n1, n2, n3, n4, n5):
    d_k1 = unpack_weight(d_words, d_scales)[np.arange(K)[:, None], runs(k1, K)]
    xq = unpack_weight(x_words, x_scales)[:, unstriped(offs)]
    a = 0.0625 * (d_k1.T @ xq)
    mb = a[:, unstriped(n1)]
    mx = mb.reshape(H, S, 4).max(axis=2)
    mn = mb.reshape(H, S, 4).min(axis=2)
    z = f64(gn) * (np.maximum(np.minimum(1.5 * a, mx), mn))
    x_two = unpack_weight(x_words, x_scales)[:, unstriped(two)]
    b = 0.0625 * (d_k1.T @ x_two)
    z2 = f64(gm) * (np.maximum(b * (sigmoid(b[np.arange(H)[:, None], runs(n2, H)])), b[np.arange(H)[:, None], runs(n3, H)]))
    h = mxq(f64(w1), 0, "e4m3").T @ mxq(z, 0, "e4m3") + mxq(f64(w2), 0, "e4m3").T @ mxq(z2, 0, "e4m3")
    return (h - h[:, unstriped(n4)]) / (np.abs(h[:, unstriped(n5)] - h) + 0.5)

@@ -1,0 +1,276 @@
+from contextlib import ExitStack
+
+import concourse.mybir as mybir
+
+K, T, S, N, G, H, W = 512, 1024, 256, 512, 2048, 512, 1024
+FLOPS = 2 * (2 * K * H * S) + 2 * (2 * H * N * S)
+
+F32 = mybir.dt.float32
+BF16 = mybir.dt.bfloat16
+I32 = mybir.dt.int32
+U32 = mybir.dt.uint32
+U16 = mybir.dt.uint16
+U8 = mybir.dt.uint8
+FP8X4 = mybir.dt.float8_e4m3fn_x4
+ALU = mybir.AluOpType
+ACT = mybir.ActivationFunctionType
+
+P = 128
+PACK = 4
+MEMBERS = 4
+HALF = S // 2
+A_WINDOW = S + 16
+B_WINDOW = 2 * S
+W_BYTES = PACK * N * 4
+
+
+def tile_picked_kjgclipgmaxfrac_none_p_kernel(
+    tc, x_words, x_scales, d_words, d_scales, gn, gm, w1, w2, offs, k1, two, n1, n2, n3, n4, n5, out
+):
+    nc = tc.nc
+    with ExitStack() as ctx:
+        keep = ctx.enter_context(tc.tile_pool(name="keep", bufs=1))
+        ring = ctx.enter_context(tc.tile_pool(name="ring", bufs=3))
+        shared = ctx.enter_context(tc.tile_pool(name="shared", bufs=1))
+        psum = ctx.enter_context(tc.psum_pool(name="psum", bufs=1))
+
+        def held(shape, dtype, name):
+            return keep.tile(shape, dtype, name=name, align_bytes=64)
+
+        def load_list(name, src):
+            tile = keep.tile(list(src.shape), U16, name=name)
+            nc.sync.dma_start(tile[:], src)
+            return tile
+
+        def as_words(packed):
+            return packed[0].rearrange("p n t -> p (n t)").bitcast(I32)
+
+        def interleave(copy, dst, src):
+            copy(dst.rearrange("p (c i) t -> p c t i", i=4), src.rearrange("p t (c i) -> p c t i", i=4))
+
+        def quantize(codes, scales, grouped):
+            nc.vector.quantize_mx(out=codes.bitcast(FP8X4), scales=scales, in_=grouped.rearrange("p c t -> p (c t)"))
+
+        d_bytes = held([P, G], U8, "d_bytes")
+        x_bytes = held([P, T], U8, "x_bytes")
+        nc.gpsimd.memset(d_bytes[:].bitcast(I32), 0)
+        nc.gpsimd.memset(x_bytes[:].bitcast(I32), 0)
+        k1_t = load_list("k1_t", k1)
+        for e in range(2):
+            nc.scalar.dma_start(d_bytes[e:P:16, :].bitcast(I32), d_scales[0, e:16:2, :].bitcast(I32))
+        two_t = load_list("two_t", two)
+        x_table = held([P, T], I32, "x_table")
+        nc.sync.dma_start(x_table[:], as_words(x_words))
+        d_table = held([P, G], I32, "d_table")
+        nc.sync.dma_start(d_table[:], as_words(d_words))
+        for s in range(4):
+            nc.scalar.dma_start(x_bytes[s:P:32, :].bitcast(I32), x_scales[0, s:16:4, :].bitcast(I32))
+        gn_t = held([P, PACK], F32, "gn_t")
+        gm_t = held([P, PACK], F32, "gm_t")
+        nc.gpsimd.dma_start(gn_t[:], gn.rearrange("(p t) o -> p (t o)", t=PACK))
+        nc.gpsimd.dma_start(gm_t[:], gm.rearrange("(p t) o -> p (t o)", t=PACK))
+        n2_t = load_list("n2_t", n2)
+        offs_t = load_list("offs_t", offs)
+        n3_t = load_list("n3_t", n3)
+        n1_t = load_list("n1_t", n1)
+        n5_t = load_list("n5_t", n5)
+        n4_t = load_list("n4_t", n4)
+
+        a_rows = [held([P, A_WINDOW], F32, f"a_rows{t}") for t in range(PACK)]
+        b_rows = [held([P, B_WINDOW], F32, f"b_rows{t}") for t in range(PACK)]
+        for tile in b_rows + a_rows:
+            nc.vector.memset(tile[:, S:], 0.0)
+        a_gain = held([P, PACK], F32, "a_gain")
+        nc.gpsimd.tensor_scalar(a_gain[:], gn_t[:], 0.0625, 0.0, ALU.mult, ALU.add)
+
+        key_bytes = held([P, H], U8, "key_bytes")
+        nc.vector.tensor_copy(key_bytes[:], d_bytes[:].indirect(k1_t[:]))
+        dealt_bytes = shared.tile([P, H], U8, name="dealt_bytes", offset=W_BYTES - H // 2)
+        nc.vector.tensor_copy(
+            dealt_bytes[:].rearrange("p (t m) -> p t m", t=PACK), key_bytes[:].rearrange("p (m t) -> p t m", t=PACK)
+        )
+        key_scales = held([P, H], U8, "key_scales")
+        nc.vector.tensor_copy(key_scales[:].bitcast(I32), dealt_bytes[:].bitcast(I32))
+        for e in range(2):
+            nc.scalar.dma_start(key_scales[2 + e : P : 32, :].bitcast(I32), dealt_bytes[16 + e : P : 32, :].bitcast(I32))
+        w_raw = []
+        for i, w in enumerate((w1, w2)):
+            raw = shared.tile([P, PACK, N], F32, name=f"w_raw{i}", offset=i * W_BYTES)
+            nc.sync.dma_start(raw[:], w.rearrange("(p t) m -> p t m", t=PACK))
+            w_raw.append(raw)
+
+        def pick_tokens(name, tokens):
+            scales = held([P, S], U8, name + "_scales")
+            nc.vector.tensor_copy(scales[:], x_bytes[:].indirect(tokens[:]))
+            codes = held([P, S], U32, name + "_codes")
+            nc.vector.tensor_copy(codes[:], x_table[:].bitcast(U32).indirect(tokens[:]))
+            return codes, scales
+
+        two_codes, two_scales = pick_tokens("two", two_t)
+        key_words = held([P, H], U32, "key_words")
+        nc.vector.tensor_copy(key_words[:], d_table[:].bitcast(U32).indirect(k1_t[:]))
+        key_codes = held([P, H], I32, "key_codes")
+        nc.vector.tensor_copy(
+            key_codes[:].rearrange("p (t c i) -> p c t i", t=PACK, i=4),
+            key_words[:].bitcast(I32).rearrange("p (c i t) -> p c t i", t=PACK, i=4),
+        )
+
+        def score(t, codes, scales, bank):
+            acc = psum.tile([P, S], F32, name=f"bank{bank}", tag=f"bank{bank}")
+            cols = slice(t * P, (t + 1) * P)
+            nc.tensor.matmul_mx(
+                out=acc[:], lhsT=key_codes[:, cols].bitcast(FP8X4), lhsT_scale=key_scales[:, cols],
+                rhs=codes[:].bitcast(FP8X4), rhs_scale=scales[:], start=True, stop=True,
+            )
+            return acc
+
+        gates = []
+        for t in range(PACK):
+            acc = score(t, two_codes, two_scales, t)
+            nc.vector.tensor_scalar(b_rows[t][:, :S], acc[:], 0.0625, None, ALU.mult)
+            gate = held([P, S], F32, f"gate{t}")
+            nc.scalar.activation(gate[:], b_rows[t][:].indirect(n2_t[:]), ACT.Sigmoid)
+            gates.append(gate)
+        idx_codes, idx_scales = pick_tokens("idx", offs_t)
+        a_acc = [score(t, idx_codes, idx_scales, PACK + t) for t in range(PACK)]
+
+        rivals = [held([P, 2, S], F32, f"rivals{pair}") for pair in range(2)]
+        for t in range(PACK):
+            nc.scalar.activation(rivals[t // 2][:, t % 2, :], b_rows[t][:].indirect(n3_t[:]), ACT.Copy)
+        for t in range(PACK):
+            nc.scalar.activation(a_rows[t][:, :S], a_acc[t][:], ACT.Copy, scale=a_gain[:, t : t + 1])
+
+        w_grouped = [held([P, N, PACK], BF16, f"w_grouped{i}") for i in range(2)]
+        w_codes = [held([P, N], U32, f"w_codes{i}") for i in range(2)]
+        w_scales = [held([P, N], U8, f"w_scales{i}") for i in range(2)]
+        z2_planes = held([P, PACK, S], BF16, "z2_planes")
+        gated = [held([P, 2, S], F32, f"gated{pair}") for pair in range(2)]
+        larger = [held([P, 2, S], F32, f"larger{pair}") for pair in range(2)]
+        for t in range(PACK):
+            nc.vector.tensor_tensor(gated[t // 2][:, t % 2, :], b_rows[t][:, :S], gates[t][:], ALU.mult)
+        interleave(nc.vector.tensor_copy, w_grouped[0][:], w_raw[0][:])
+        for pair in range(2):
+            nc.vector.tensor_tensor(larger[pair][:], gated[pair][:], rivals[pair][:], ALU.max)
+        for t in range(PACK):
+            nc.vector.tensor_scalar(z2_planes[:, t, :], larger[t // 2][:, t % 2, :], gm_t[:, t : t + 1], None, ALU.mult)
+        z2_grouped = held([P, S, PACK], BF16, "z2_grouped")
+        quantize(w_codes[0][:], w_scales[0][:], w_grouped[0][:])
+        interleave(nc.vector.tensor_copy, z2_grouped[:], z2_planes[:])
+        z2_codes = held([P, S], U32, "z2_codes")
+        z2_scales = held([P, S], U8, "z2_scales")
+
+        z_pairs = [held([P, 2, HALF, 2], BF16, f"z_pairs{half}") for half in range(2)]
+        z_grouped = [held([P, HALF, PACK], BF16, f"z_grouped{half}") for half in range(2)]
+        z_codes = [held([P, HALF], U32, f"z_codes{half}") for half in range(2)]
+        z_scales = [held([P, HALF], U8, f"z_scales{half}") for half in range(2)]
+
+        def clip_first(half, pair):
+            members = held([P, 2, HALF * MEMBERS], F32, f"members{half}{pair}")
+            for e in range(2):
+                for c in range(2):
+                    col = (2 * half + c) * 16
+                    nc.scalar.activation(
+                        members[:, e, c * S : (c + 1) * S], a_rows[2 * pair + e][:].indirect(n1_t[:, col : col + 16]), ACT.Copy
+                    )
+            quads = members[:].rearrange("p e (j m) -> p (e j) m", m=MEMBERS)
+            highs = ring.tile([P, 2 * HALF, 2], F32, name="highs")
+            lows = ring.tile([P, 2 * HALF, 2], F32, name="lows")
+            nc.vector.tensor_tensor(highs[:], quads[:, :, 0:2], quads[:, :, 2:4], ALU.max)
+            nc.vector.tensor_tensor(lows[:], quads[:, :, 0:2], quads[:, :, 2:4], ALU.min)
+            return highs, lows
+
+        def clip_second(half, pair, highs, lows):
+            high = ring.tile([P, 2, HALF], F32, name="high")
+            low = ring.tile([P, 2, HALF], F32, name="low")
+            capped = ring.tile([P, 2, HALF], F32, name="capped")
+            nc.vector.tensor_tensor(high[:].rearrange("p e j -> p (e j)"), highs[:, :, 0], highs[:, :, 1], ALU.max)
+            nc.vector.tensor_tensor(low[:].rearrange("p e j -> p (e j)"), lows[:, :, 0], lows[:, :, 1], ALU.min)
+            for e in range(2):
+                nc.vector.scalar_tensor_tensor(
+                    capped[:, e, :], a_rows[2 * pair + e][:, half * HALF : (half + 1) * HALF], 1.5, high[:, e, :], ALU.mult, ALU.min
+                )
+            return capped, low
+
+        def clip_last(half, pair, capped, low):
+            nc.vector.tensor_tensor(
+                z_pairs[half][:, pair, :, :], capped[:].rearrange("p e j -> p j e"), low[:].rearrange("p e j -> p j e"), ALU.max
+            )
+
+        def weave(half):
+            nc.vector.tensor_copy(
+                z_grouped[half][:].rearrange("p j t -> p (j t)").bitcast(F32).rearrange("p (j w) -> p j w", w=2),
+                z_pairs[half][:].rearrange("p w j e -> p (w j e)").bitcast(F32).rearrange("p (w j) -> p j w", w=2),
+            )
+
+        units = [(half, pair) for half in range(2) for pair in range(2)]
+        pending = None
+        for n, (half, pair) in enumerate(units):
+            highs, lows = clip_first(half, pair)
+            if pending is not None:
+                clip_last(*pending)
+            if n == 0:
+                quantize(z2_codes[:], z2_scales[:], z2_grouped[:])
+            pending = (half, pair) + clip_second(half, pair, highs, lows)
+            if n == 2:
+                weave(0)
+            if n == 3:
+                quantize(z_codes[0][:], z_scales[0][:], z_grouped[0][:])
+        clip_last(*pending)
+        weave(1)
+        interleave(nc.scalar.copy, w_grouped[1][:], w_raw[1][:])
+        quantize(z_codes[1][:], z_scales[1][:], z_grouped[1][:])
+        quantize(w_codes[1][:], w_scales[1][:], w_grouped[1][:])
+
+        h_rows = b_rows
+        for u in range(N // P):
+            acc = psum.tile([P, S], F32, name=f"bank{u}", tag=f"bank{u}")
+            cols = slice(u * P, (u + 1) * P)
+            for half in range(2):
+                nc.tensor.matmul_mx(
+                    out=acc[:, half * HALF : (half + 1) * HALF], lhsT=w_codes[0][:, cols].bitcast(FP8X4),
+                    lhsT_scale=w_scales[0][:, cols], rhs=z_codes[half][:].bitcast(FP8X4),
+                    rhs_scale=z_scales[half][:], start=(half == 0), stop=False,
+                )
+            nc.tensor.matmul_mx(
+                out=acc[:], lhsT=w_codes[1][:, cols].bitcast(FP8X4), lhsT_scale=w_scales[1][:, cols],
+                rhs=z2_codes[:].bitcast(FP8X4), rhs_scale=z2_scales[:], start=False, stop=True,
+            )
+            nc.vector.tensor_copy(h_rows[u][:, :S], acc[:])
+        names = ("at_n5", "at_n4", "diff", "dist", "numer", "root", "once", "quot")
+        at_n5, at_n4, diff, dist, numer, root, once, quot = (
+            [held([P, S], F32, f"{name}{u}") for u in range(N // P)] for name in names
+        )
+
+        def distance(u):
+            nc.scalar.activation(at_n5[u][:], h_rows[u][:].indirect(n5_t[:]), ACT.Copy)
+            nc.vector.tensor_tensor(diff[u][:], at_n5[u][:], h_rows[u][:, :S], ALU.subtract)
+
+        def magnitude(u):
+            nc.vector.scalar_tensor_tensor(dist[u][:], diff[u][:], -1.0, diff[u][:], ALU.mult, ALU.max)
+
+        def numerator(u):
+            nc.scalar.activation(at_n4[u][:], h_rows[u][:].indirect(n4_t[:]), ACT.Copy)
+            nc.vector.tensor_tensor(numer[u][:], h_rows[u][:, :S], at_n4[u][:], ALU.subtract)
+
+        def divide_once(u):
+            nc.scalar.activation(root[u][:], dist[u][:], ACT.Abs_reciprocal_sqrt, bias=0.5)
+            nc.vector.tensor_tensor(once[u][:], numer[u][:], root[u][:], ALU.mult)
+
+        def divide_twice(u):
+            nc.vector.tensor_tensor(quot[u][:], once[u][:], root[u][:], ALU.mult)
+            nc.sync.dma_start(out[u * P : (u + 1) * P, :], quot[u][:])
+
+        blocks = N // P
+        distance(0)
+        magnitude(0)
+        for u in range(blocks + 1):
+            if u + 1 < blocks:
+                distance(u + 1)
+            if u > 0:
+                divide_twice(u - 1)
+            if u < blocks:
+                numerator(u)
+            if u + 1 < blocks:
+                magnitude(u + 1)
+            if u < blocks:
+                divide_once(u)

@@ -19,9 +19,10 @@ P = 128
 PACK = 4
 MEMBERS = 4
 HALF = S // 2
-A_WINDOW = S + 16
+A_WINDOW = 2 * S + 16
 B_WINDOW = 2 * S
 W_BYTES = PACK * N * 4
+SQUARED_ON_SCALAR = 2
 
 
 def tile_picked_kjgclipgmaxfrac_none_p_kernel(
@@ -35,7 +36,7 @@ def tile_picked_kjgclipgmaxfrac_none_p_kernel(
         psum = ctx.enter_context(tc.psum_pool(name="psum", bufs=1))
 
         def held(shape, dtype, name):
-            return keep.tile(shape, dtype, name=name, align_bytes=64)
+            return keep.tile(shape, dtype, name=name, tag=name, align_bytes=64)
 
         def load_list(name, src):
             tile = keep.tile(list(src.shape), U16, name=name)
@@ -46,33 +47,37 @@ def tile_picked_kjgclipgmaxfrac_none_p_kernel(
             return packed[0].rearrange("p n t -> p (n t)").bitcast(I32)
 
         def interleave(copy, dst, src):
-            copy(dst.rearrange("p (c i) t -> p c t i", i=4), src.rearrange("p t (c i) -> p c t i", i=4))
+            copy(dst, src.rearrange("p t c -> p c t"))
 
         def quantize(codes, scales, grouped):
             nc.vector.quantize_mx(out=codes.bitcast(FP8X4), scales=scales, in_=grouped.rearrange("p c t -> p (c t)"))
 
         d_bytes = held([P, G], U8, "d_bytes")
         x_bytes = held([P, T], U8, "x_bytes")
-        nc.gpsimd.memset(d_bytes[:].bitcast(I32), 0)
+        nc.vector.memset(d_bytes[:].bitcast(I32), 0)
         nc.gpsimd.memset(x_bytes[:].bitcast(I32), 0)
+        def load_weights(w, side, raw):
+            nc.sync.dma_start(raw[:], w.rearrange("(p t) m -> p t m", t=PACK)[:, :, side * N // 2 : (side + 1) * N // 2])
+            return raw
+
+        w1_raw = [load_weights(w1, 0, held([P, PACK, N // 2], F32, "w1_raw0"))]
         k1_t = load_list("k1_t", k1)
-        for e in range(2):
-            nc.scalar.dma_start(d_bytes[e:P:16, :].bitcast(I32), d_scales[0, e:16:2, :].bitcast(I32))
+        nc.sync.dma_start(d_bytes[0:P:8, :].bitcast(I32), d_scales[0].bitcast(I32))
+        nc.sync.dma_start(x_bytes[0:P:8, :].bitcast(I32), x_scales[0].bitcast(I32))
+        offs_t = load_list("offs_t", offs)
         two_t = load_list("two_t", two)
+        d_table = shared.tile([P, G], I32, name="d_table", offset=0)
+        nc.sync.dma_start(d_table[:], as_words(d_words))
         x_table = held([P, T], I32, "x_table")
         nc.sync.dma_start(x_table[:], as_words(x_words))
-        d_table = held([P, G], I32, "d_table")
-        nc.sync.dma_start(d_table[:], as_words(d_words))
-        for s in range(4):
-            nc.scalar.dma_start(x_bytes[s:P:32, :].bitcast(I32), x_scales[0, s:16:4, :].bitcast(I32))
         gn_t = held([P, PACK], F32, "gn_t")
         gm_t = held([P, PACK], F32, "gm_t")
-        nc.gpsimd.dma_start(gn_t[:], gn.rearrange("(p t) o -> p (t o)", t=PACK))
-        nc.gpsimd.dma_start(gm_t[:], gm.rearrange("(p t) o -> p (t o)", t=PACK))
-        n2_t = load_list("n2_t", n2)
-        offs_t = load_list("offs_t", offs)
-        n3_t = load_list("n3_t", n3)
+        nc.sync.dma_start(gn_t[:], gn.rearrange("(p t) o -> p (t o)", t=PACK))
+        nc.sync.dma_start(gm_t[:], gm.rearrange("(p t) o -> p (t o)", t=PACK))
         n1_t = load_list("n1_t", n1)
+        n2_t = load_list("n2_t", n2)
+        n3_t = load_list("n3_t", n3)
+        w1_raw.append(load_weights(w1, 1, held([P, PACK, N // 2], F32, "w1_raw1")))
         n5_t = load_list("n5_t", n5)
         n4_t = load_list("n4_t", n4)
 
@@ -80,33 +85,25 @@ def tile_picked_kjgclipgmaxfrac_none_p_kernel(
         b_rows = [held([P, B_WINDOW], F32, f"b_rows{t}") for t in range(PACK)]
         for tile in b_rows + a_rows:
             nc.vector.memset(tile[:, S:], 0.0)
+        warm = held([P, 2], F32, "warm")
+        nc.scalar.activation(warm[:, 0:1], b_rows[0][:, S : S + 1], ACT.Sigmoid)
+        planes = held([P, H + 2 * S], U8, "planes")
+        nc.vector.memset(planes[:].bitcast(I32), 0)
         a_gain = held([P, PACK], F32, "a_gain")
+        b_gain = held([P, PACK], F32, "b_gain")
+        cap_gain = held([P, PACK], F32, "cap_gain")
+        nc.gpsimd.tensor_scalar(cap_gain[:], gn_t[:], 1.5 * 0.0625, 0.0, ALU.mult, ALU.add)
         nc.gpsimd.tensor_scalar(a_gain[:], gn_t[:], 0.0625, 0.0, ALU.mult, ALU.add)
+        nc.gpsimd.tensor_scalar(b_gain[:], gm_t[:], 0.0625, 0.0, ALU.mult, ALU.add)
 
-        key_bytes = held([P, H], U8, "key_bytes")
-        nc.vector.tensor_copy(key_bytes[:], d_bytes[:].indirect(k1_t[:]))
-        dealt_bytes = shared.tile([P, H], U8, name="dealt_bytes", offset=W_BYTES - H // 2)
-        nc.vector.tensor_copy(
-            dealt_bytes[:].rearrange("p (t m) -> p t m", t=PACK), key_bytes[:].rearrange("p (m t) -> p t m", t=PACK)
-        )
-        key_scales = held([P, H], U8, "key_scales")
-        nc.vector.tensor_copy(key_scales[:].bitcast(I32), dealt_bytes[:].bitcast(I32))
-        for e in range(2):
-            nc.scalar.dma_start(key_scales[2 + e : P : 32, :].bitcast(I32), dealt_bytes[16 + e : P : 32, :].bitcast(I32))
-        w_raw = []
-        for i, w in enumerate((w1, w2)):
-            raw = shared.tile([P, PACK, N], F32, name=f"w_raw{i}", offset=i * W_BYTES)
-            nc.sync.dma_start(raw[:], w.rearrange("(p t) m -> p t m", t=PACK))
-            w_raw.append(raw)
+        picked_bytes = held([P, H + 2 * S], U8, "picked_bytes")
+        nc.vector.tensor_copy(picked_bytes[:, :H], d_bytes[:].indirect(k1_t[:]))
+        nc.vector.tensor_copy(picked_bytes[:, H : H + S], x_bytes[:].indirect(two_t[:]))
+        nc.vector.tensor_copy(picked_bytes[:, H + S :], x_bytes[:].indirect(offs_t[:]))
+        for s in range(4):
+            nc.scalar.dma_start(planes[s:P:32, :].bitcast(I32), picked_bytes[8 * s : P : 32, :].bitcast(I32))
+        two_scales, idx_scales = planes[:, H : H + S], planes[:, H + S :]
 
-        def pick_tokens(name, tokens):
-            scales = held([P, S], U8, name + "_scales")
-            nc.vector.tensor_copy(scales[:], x_bytes[:].indirect(tokens[:]))
-            codes = held([P, S], U32, name + "_codes")
-            nc.vector.tensor_copy(codes[:], x_table[:].bitcast(U32).indirect(tokens[:]))
-            return codes, scales
-
-        two_codes, two_scales = pick_tokens("two", two_t)
         key_words = held([P, H], U32, "key_words")
         nc.vector.tensor_copy(key_words[:], d_table[:].bitcast(U32).indirect(k1_t[:]))
         key_codes = held([P, H], I32, "key_codes")
@@ -114,48 +111,57 @@ def tile_picked_kjgclipgmaxfrac_none_p_kernel(
             key_codes[:].rearrange("p (t c i) -> p c t i", t=PACK, i=4),
             key_words[:].bitcast(I32).rearrange("p (c i t) -> p c t i", t=PACK, i=4),
         )
+        key_scales = held([P, H], U8, "key_scales")
+        nc.vector.tensor_copy(
+            key_scales[:].rearrange("p (t m) -> p t m", t=PACK), planes[:, :H].rearrange("p (m t) -> p t m", t=PACK)
+        )
+        idx_codes = held([P, S], U32, "idx_codes")
+        nc.vector.tensor_copy(idx_codes[:], x_table[:].bitcast(U32).indirect(offs_t[:]))
+        two_codes = held([P, S], U32, "two_codes")
+        nc.vector.tensor_copy(two_codes[:], x_table[:].bitcast(U32).indirect(two_t[:]))
+
+        w2_raw = [
+            load_weights(w2, side, shared.tile([P, PACK, N // 2], F32, name=f"w2_raw{side}", offset=side * W_BYTES // 2))
+            for side in range(2)
+        ]
+        w_grouped = [held([P, N, PACK], BF16, f"w_grouped{i}") for i in range(2)]
+        for side in range(2):
+            interleave(nc.scalar.copy, w_grouped[0][:, side * N // 2 : (side + 1) * N // 2, :], w1_raw[side][:])
 
         def score(t, codes, scales, bank):
             acc = psum.tile([P, S], F32, name=f"bank{bank}", tag=f"bank{bank}")
             cols = slice(t * P, (t + 1) * P)
             nc.tensor.matmul_mx(
                 out=acc[:], lhsT=key_codes[:, cols].bitcast(FP8X4), lhsT_scale=key_scales[:, cols],
-                rhs=codes[:].bitcast(FP8X4), rhs_scale=scales[:], start=True, stop=True,
+                rhs=codes[:].bitcast(FP8X4), rhs_scale=scales, start=True, stop=True,
             )
             return acc
 
-        gates = []
-        for t in range(PACK):
-            acc = score(t, two_codes, two_scales, t)
-            nc.vector.tensor_scalar(b_rows[t][:, :S], acc[:], 0.0625, None, ALU.mult)
-            gate = held([P, S], F32, f"gate{t}")
-            nc.scalar.activation(gate[:], b_rows[t][:].indirect(n2_t[:]), ACT.Sigmoid)
-            gates.append(gate)
-        idx_codes, idx_scales = pick_tokens("idx", offs_t)
-        a_acc = [score(t, idx_codes, idx_scales, PACK + t) for t in range(PACK)]
+        gates = [held([P, S], F32, f"gate{t}") for t in range(PACK)]
+        gated = [held([P, 2, S], F32, f"gated{pair}") for pair in range(2)]
 
-        rivals = [held([P, 2, S], F32, f"rivals{pair}") for pair in range(2)]
-        for t in range(PACK):
-            nc.scalar.activation(rivals[t // 2][:, t % 2, :], b_rows[t][:].indirect(n3_t[:]), ACT.Copy)
-        for t in range(PACK):
-            nc.scalar.activation(a_rows[t][:, :S], a_acc[t][:], ACT.Copy, scale=a_gain[:, t : t + 1])
+        def gate_rows(t):
+            nc.scalar.copy(b_rows[t][:, :S], score(t, two_codes, two_scales, t)[:])
+            nc.scalar.activation(gates[t][:], b_rows[t][:].indirect(n2_t[:]), ACT.Sigmoid, scale=0.0625)
 
-        w_grouped = [held([P, N, PACK], BF16, f"w_grouped{i}") for i in range(2)]
+        def apply_gate(t):
+            nc.vector.tensor_tensor(gated[t // 2][:, t % 2, :], b_rows[t][:, :S], gates[t][:], ALU.mult)
+
+
+        a_banks = [score(t, idx_codes, idx_scales, t) for t in range(PACK)]
+        for t, acc in enumerate(a_banks):
+            if t == 0:
+                nc.scalar.activation(a_rows[t][:, :S], acc[:], ACT.Copy, scale=a_gain[:, t : t + 1])
+            else:
+                nc.vector.tensor_scalar(a_rows[t][:, :S], acc[:], a_gain[:, t : t + 1], None, ALU.mult)
         w_codes = [held([P, N], U32, f"w_codes{i}") for i in range(2)]
         w_scales = [held([P, N], U8, f"w_scales{i}") for i in range(2)]
-        z2_planes = held([P, PACK, S], BF16, "z2_planes")
-        gated = [held([P, 2, S], F32, f"gated{pair}") for pair in range(2)]
-        larger = [held([P, 2, S], F32, f"larger{pair}") for pair in range(2)]
-        for t in range(PACK):
-            nc.vector.tensor_tensor(gated[t // 2][:, t % 2, :], b_rows[t][:, :S], gates[t][:], ALU.mult)
-        interleave(nc.vector.tensor_copy, w_grouped[0][:], w_raw[0][:])
-        for pair in range(2):
-            nc.vector.tensor_tensor(larger[pair][:], gated[pair][:], rivals[pair][:], ALU.max)
-        for t in range(PACK):
-            nc.vector.tensor_scalar(z2_planes[:, t, :], larger[t // 2][:, t % 2, :], gm_t[:, t : t + 1], None, ALU.mult)
-        z2_grouped = held([P, S, PACK], BF16, "z2_grouped")
         quantize(w_codes[0][:], w_scales[0][:], w_grouped[0][:])
-        interleave(nc.vector.tensor_copy, z2_grouped[:], z2_planes[:])
+        for side in range(2):
+            interleave(nc.vector.tensor_copy, w_grouped[1][:, side * N // 2 : (side + 1) * N // 2, :], w2_raw[side][:])
+
+        z2_planes = held([P, PACK, S], BF16, "z2_planes")
+        z2_grouped = held([P, S, PACK], BF16, "z2_grouped")
         z2_codes = held([P, S], U32, "z2_codes")
         z2_scales = held([P, S], U8, "z2_scales")
 
@@ -164,32 +170,29 @@ def tile_picked_kjgclipgmaxfrac_none_p_kernel(
         z_codes = [held([P, HALF], U32, f"z_codes{half}") for half in range(2)]
         z_scales = [held([P, HALF], U8, f"z_scales{half}") for half in range(2)]
 
-        def clip_first(half, pair):
+        def fetch_members(half, pair):
             members = held([P, 2, HALF * MEMBERS], F32, f"members{half}{pair}")
             for e in range(2):
-                for c in range(2):
-                    col = (2 * half + c) * 16
-                    nc.scalar.activation(
-                        members[:, e, c * S : (c + 1) * S], a_rows[2 * pair + e][:].indirect(n1_t[:, col : col + 16]), ACT.Copy
-                    )
-            quads = members[:].rearrange("p e (j m) -> p (e j) m", m=MEMBERS)
-            highs = ring.tile([P, 2 * HALF, 2], F32, name="highs")
-            lows = ring.tile([P, 2 * HALF, 2], F32, name="lows")
-            nc.vector.tensor_tensor(highs[:], quads[:, :, 0:2], quads[:, :, 2:4], ALU.max)
-            nc.vector.tensor_tensor(lows[:], quads[:, :, 0:2], quads[:, :, 2:4], ALU.min)
-            return highs, lows
-
-        def clip_second(half, pair, highs, lows):
-            high = ring.tile([P, 2, HALF], F32, name="high")
-            low = ring.tile([P, 2, HALF], F32, name="low")
-            capped = ring.tile([P, 2, HALF], F32, name="capped")
-            nc.vector.tensor_tensor(high[:].rearrange("p e j -> p (e j)"), highs[:, :, 0], highs[:, :, 1], ALU.max)
-            nc.vector.tensor_tensor(low[:].rearrange("p e j -> p (e j)"), lows[:, :, 0], lows[:, :, 1], ALU.min)
-            for e in range(2):
-                nc.vector.scalar_tensor_tensor(
-                    capped[:, e, :], a_rows[2 * pair + e][:, half * HALF : (half + 1) * HALF], 1.5, high[:, e, :], ALU.mult, ALU.min
+                nc.scalar.activation(
+                    members[:, e, :], a_rows[2 * pair + e][:].indirect(n1_t[:, 32 * half : 32 * (half + 1)]), ACT.Copy
                 )
-            return capped, low
+            return members
+
+        def clip_first(members, tiles, highs, lows):
+            quads = members[:, tiles, :].rearrange("p e (j m) -> p (e j) m", m=MEMBERS)
+            for op, dst in ((ALU.max, highs), (ALU.min, lows)):
+                nc.vector.tensor_tensor(dst[:, tiles, :, :].rearrange("p e j m -> p (e j) m"), quads[:, :, 0:2], quads[:, :, 2:4], op)
+
+        def clip_second(half, pair, tiles, highs, lows, high, low, capped):
+            for op, dst, src in ((ALU.max, high, highs), (ALU.min, low, lows)):
+                nc.vector.tensor_tensor(dst[:, tiles, :], src[:, tiles, :, 0], src[:, tiles, :, 1], op)
+            for e in range(tiles.start, tiles.stop):
+                t = 2 * pair + e
+                if half == 0:
+                    own, factor = a_banks[t][:, :HALF], cap_gain[:, t : t + 1]
+                else:
+                    own, factor = a_rows[t][:, HALF:S], 1.5
+                nc.vector.scalar_tensor_tensor(capped[:, e, :], own, factor, high[:, e, :], ALU.mult, ALU.min)
 
         def clip_last(half, pair, capped, low):
             nc.vector.tensor_tensor(
@@ -205,25 +208,56 @@ def tile_picked_kjgclipgmaxfrac_none_p_kernel(
         units = [(half, pair) for half in range(2) for pair in range(2)]
         pending = None
         for n, (half, pair) in enumerate(units):
-            highs, lows = clip_first(half, pair)
+            members = fetch_members(half, pair)
+            highs = shared.tile([P, 2, HALF, 2], F32, name=f"highs{n}", offset=(n % 2) * W_BYTES // 4)
+            lows = shared.tile([P, 2, HALF, 2], F32, name=f"lows{n}", offset=(2 + n % 2) * W_BYTES // 4)
+            high = ring.tile([P, 2, HALF], F32, name="high")
+            low = ring.tile([P, 2, HALF], F32, name="low")
+            capped = ring.tile([P, 2, HALF], F32, name="capped")
+            tiles = slice(0, 2)
+            clip_first(members, tiles, highs, lows)
             if pending is not None:
                 clip_last(*pending)
+            clip_second(half, pair, tiles, highs, lows, high, low, capped)
+            pending = (half, pair, capped, low)
             if n == 0:
-                quantize(z2_codes[:], z2_scales[:], z2_grouped[:])
-            pending = (half, pair) + clip_second(half, pair, highs, lows)
+                quantize(w_codes[1][:], w_scales[1][:], w_grouped[1][:])
             if n == 2:
                 weave(0)
             if n == 3:
                 quantize(z_codes[0][:], z_scales[0][:], z_grouped[0][:])
         clip_last(*pending)
+
+        rival = [held([P, S], F32, f"rival{t}") for t in range(PACK)]
+        larger = [held([P, 2, S], F32, f"larger{pair}") for pair in range(2)]
+
+        def take_larger(t):
+            nc.scalar.activation(rival[t][:], b_rows[t][:].indirect(n3_t[:]), ACT.Copy)
+            nc.vector.tensor_tensor(larger[t // 2][:, t % 2, :], gated[t // 2][:, t % 2, :], rival[t][:], ALU.max)
+
+        def apply_gain(t):
+            nc.vector.tensor_scalar(z2_planes[:, t, :], larger[t // 2][:, t % 2, :], b_gain[:, t : t + 1], None, ALU.mult)
+
+        for t in range(PACK):
+            gate_rows(t)
+        apply_gate(0)
         weave(1)
-        interleave(nc.scalar.copy, w_grouped[1][:], w_raw[1][:])
+        apply_gate(1)
+        apply_gate(2)
         quantize(z_codes[1][:], z_scales[1][:], z_grouped[1][:])
-        quantize(w_codes[1][:], w_scales[1][:], w_grouped[1][:])
+        apply_gate(3)
+        for t in range(PACK + 1):
+            if t < PACK:
+                take_larger(t)
+            if t > 0:
+                apply_gain(t - 1)
+        interleave(nc.vector.tensor_copy, z2_grouped[:], z2_planes[:])
+        nc.scalar.activation(warm[:, 1:2], rival[PACK - 1][:, 0:1], ACT.Abs_reciprocal_sqrt, bias=0.5, scale=0.0)
+        quantize(z2_codes[:], z2_scales[:], z2_grouped[:])
 
         h_rows = b_rows
         for u in range(N // P):
-            acc = psum.tile([P, S], F32, name=f"bank{u}", tag=f"bank{u}")
+            acc = psum.tile([P, S], F32, name=f"bank{PACK + u}", tag=f"bank{PACK + u}")
             cols = slice(u * P, (u + 1) * P)
             for half in range(2):
                 nc.tensor.matmul_mx(
@@ -254,10 +288,13 @@ def tile_picked_kjgclipgmaxfrac_none_p_kernel(
 
         def divide_once(u):
             nc.scalar.activation(root[u][:], dist[u][:], ACT.Abs_reciprocal_sqrt, bias=0.5)
-            nc.vector.tensor_tensor(once[u][:], numer[u][:], root[u][:], ALU.mult)
+            if u < SQUARED_ON_SCALAR:
+                nc.scalar.activation(once[u][:], root[u][:], ACT.Square)
+            else:
+                nc.vector.tensor_tensor(once[u][:], root[u][:], root[u][:], ALU.mult)
 
         def divide_twice(u):
-            nc.vector.tensor_tensor(quot[u][:], once[u][:], root[u][:], ALU.mult)
+            nc.vector.tensor_tensor(quot[u][:], once[u][:], numer[u][:], ALU.mult)
             nc.sync.dma_start(out[u * P : (u + 1) * P, :], quot[u][:])
 
         blocks = N // P

@@ -2,7 +2,7 @@ from contextlib import ExitStack
 
 import concourse.mybir as mybir
 
-K, T, S, N, G, H, W = 512, 1024, 256, 512, 2048, 512, 1024
+K, T, S, N, G, H = 512, 1024, 256, 512, 2048, 512
 FLOPS = 2 * (2 * K * H * S) + 2 * (2 * H * N * S)
 
 F32 = mybir.dt.float32
@@ -17,11 +17,16 @@ ACT = mybir.ActivationFunctionType
 
 P = 128
 PACK = 4
+QUADRANT = 32
+BLOCK_PARTITIONS = 8
+LIST_ROWS = 16
 MEMBERS = 4
 HALF = S // 2
-A_WINDOW = 2 * S + 16
+SIDE = N // 2
+SIDE_BYTES = PACK * SIDE * 4
+SIXTEENTH = 0.0625
+A_WINDOW = HALF * MEMBERS + LIST_ROWS
 B_WINDOW = 2 * S
-W_BYTES = PACK * N * 4
 SQUARED_ON_SCALAR = 2
 
 
@@ -46,6 +51,10 @@ def tile_picked_kjgclipgmaxfrac_none_p_kernel(
         def as_words(packed):
             return packed[0].rearrange("p n t -> p (n t)").bitcast(I32)
 
+        def load_weights(w, side, raw):
+            nc.sync.dma_start(raw[:], w.rearrange("(p t) m -> p t m", t=PACK)[:, :, side * SIDE : (side + 1) * SIDE])
+            return raw
+
         def interleave(copy, dst, src):
             copy(dst, src.rearrange("p t c -> p c t"))
 
@@ -56,19 +65,15 @@ def tile_picked_kjgclipgmaxfrac_none_p_kernel(
         x_bytes = held([P, T], U8, "x_bytes")
         nc.vector.memset(d_bytes[:].bitcast(I32), 0)
         nc.gpsimd.memset(x_bytes[:].bitcast(I32), 0)
-        def load_weights(w, side, raw):
-            nc.sync.dma_start(raw[:], w.rearrange("(p t) m -> p t m", t=PACK)[:, :, side * N // 2 : (side + 1) * N // 2])
-            return raw
-
-        w1_raw = [load_weights(w1, 0, held([P, PACK, N // 2], F32, "w1_raw0"))]
+        w1_left = load_weights(w1, 0, held([P, PACK, SIDE], F32, "w1_left"))
         k1_t = load_list("k1_t", k1)
-        nc.sync.dma_start(d_bytes[0:P:8, :].bitcast(I32), d_scales[0].bitcast(I32))
-        nc.sync.dma_start(x_bytes[0:P:8, :].bitcast(I32), x_scales[0].bitcast(I32))
+        nc.sync.dma_start(d_bytes[0:P:BLOCK_PARTITIONS, :].bitcast(I32), d_scales[0].bitcast(I32))
+        nc.sync.dma_start(x_bytes[0:P:BLOCK_PARTITIONS, :].bitcast(I32), x_scales[0].bitcast(I32))
         offs_t = load_list("offs_t", offs)
         two_t = load_list("two_t", two)
         d_table = shared.tile([P, G], I32, name="d_table", offset=0)
         nc.sync.dma_start(d_table[:], as_words(d_words))
-        x_table = held([P, T], I32, "x_table")
+        x_table = shared.tile([P, T], I32, name="x_table", offset=2 * SIDE_BYTES)
         nc.sync.dma_start(x_table[:], as_words(x_words))
         gn_t = held([P, PACK], F32, "gn_t")
         gm_t = held([P, PACK], F32, "gm_t")
@@ -77,7 +82,6 @@ def tile_picked_kjgclipgmaxfrac_none_p_kernel(
         n1_t = load_list("n1_t", n1)
         n2_t = load_list("n2_t", n2)
         n3_t = load_list("n3_t", n3)
-        w1_raw.append(load_weights(w1, 1, held([P, PACK, N // 2], F32, "w1_raw1")))
         n5_t = load_list("n5_t", n5)
         n4_t = load_list("n4_t", n4)
 
@@ -87,22 +91,24 @@ def tile_picked_kjgclipgmaxfrac_none_p_kernel(
             nc.vector.memset(tile[:, S:], 0.0)
         warm = held([P, 2], F32, "warm")
         nc.scalar.activation(warm[:, 0:1], b_rows[0][:, S : S + 1], ACT.Sigmoid)
-        planes = held([P, H + 2 * S], U8, "planes")
-        nc.vector.memset(planes[:].bitcast(I32), 0)
+        scale_rows = held([P, H + 2 * S], U8, "scale_rows")
+        nc.vector.memset(scale_rows[:].bitcast(I32), 0)
         a_gain = held([P, PACK], F32, "a_gain")
         b_gain = held([P, PACK], F32, "b_gain")
         cap_gain = held([P, PACK], F32, "cap_gain")
-        nc.gpsimd.tensor_scalar(cap_gain[:], gn_t[:], 1.5 * 0.0625, 0.0, ALU.mult, ALU.add)
-        nc.gpsimd.tensor_scalar(a_gain[:], gn_t[:], 0.0625, 0.0, ALU.mult, ALU.add)
-        nc.gpsimd.tensor_scalar(b_gain[:], gm_t[:], 0.0625, 0.0, ALU.mult, ALU.add)
+        nc.gpsimd.tensor_scalar(cap_gain[:], gn_t[:], 1.5 * SIXTEENTH, 0.0, ALU.mult, ALU.add)
+        nc.gpsimd.tensor_scalar(a_gain[:], gn_t[:], SIXTEENTH, 0.0, ALU.mult, ALU.add)
+        nc.gpsimd.tensor_scalar(b_gain[:], gm_t[:], SIXTEENTH, 0.0, ALU.mult, ALU.add)
 
         picked_bytes = held([P, H + 2 * S], U8, "picked_bytes")
         nc.vector.tensor_copy(picked_bytes[:, :H], d_bytes[:].indirect(k1_t[:]))
         nc.vector.tensor_copy(picked_bytes[:, H : H + S], x_bytes[:].indirect(two_t[:]))
         nc.vector.tensor_copy(picked_bytes[:, H + S :], x_bytes[:].indirect(offs_t[:]))
-        for s in range(4):
-            nc.scalar.dma_start(planes[s:P:32, :].bitcast(I32), picked_bytes[8 * s : P : 32, :].bitcast(I32))
-        two_scales, idx_scales = planes[:, H : H + S], planes[:, H + S :]
+        for s in range(QUADRANT // BLOCK_PARTITIONS):
+            nc.scalar.dma_start(
+                scale_rows[s:P:QUADRANT, :].bitcast(I32), picked_bytes[BLOCK_PARTITIONS * s : P : QUADRANT, :].bitcast(I32)
+            )
+        two_scales, idx_scales = scale_rows[:, H : H + S], scale_rows[:, H + S :]
 
         key_words = held([P, H], U32, "key_words")
         nc.vector.tensor_copy(key_words[:], d_table[:].bitcast(U32).indirect(k1_t[:]))
@@ -113,23 +119,22 @@ def tile_picked_kjgclipgmaxfrac_none_p_kernel(
         )
         key_scales = held([P, H], U8, "key_scales")
         nc.vector.tensor_copy(
-            key_scales[:].rearrange("p (t m) -> p t m", t=PACK), planes[:, :H].rearrange("p (m t) -> p t m", t=PACK)
+            key_scales[:].rearrange("p (t m) -> p t m", t=PACK), scale_rows[:, :H].rearrange("p (m t) -> p t m", t=PACK)
         )
         idx_codes = held([P, S], U32, "idx_codes")
         nc.vector.tensor_copy(idx_codes[:], x_table[:].bitcast(U32).indirect(offs_t[:]))
         two_codes = held([P, S], U32, "two_codes")
         nc.vector.tensor_copy(two_codes[:], x_table[:].bitcast(U32).indirect(two_t[:]))
 
-        w2_raw = [
-            load_weights(w2, side, shared.tile([P, PACK, N // 2], F32, name=f"w2_raw{side}", offset=side * W_BYTES // 2))
-            for side in range(2)
-        ]
-        w_grouped = [held([P, N, PACK], BF16, f"w_grouped{i}") for i in range(2)]
-        for side in range(2):
-            interleave(nc.scalar.copy, w_grouped[0][:, side * N // 2 : (side + 1) * N // 2, :], w1_raw[side][:])
+        w1_right, w2_left, w2_right = (
+            load_weights(w, side, shared.tile([P, PACK, SIDE], F32, name=f"w_raw{n}", offset=n * SIDE_BYTES))
+            for n, (w, side) in enumerate(((w1, 1), (w2, 0), (w2, 1)))
+        )
+        w1_grouped = held([P, N, PACK], BF16, "w1_grouped")
+        interleave(nc.scalar.copy, w1_grouped[:, :SIDE, :], w1_left[:])
 
-        def score(t, codes, scales, bank):
-            acc = psum.tile([P, S], F32, name=f"bank{bank}", tag=f"bank{bank}")
+        def score(t, codes, scales):
+            acc = psum.tile([P, S], F32, name=f"bank{t}", tag=f"bank{t}")
             cols = slice(t * P, (t + 1) * P)
             nc.tensor.matmul_mx(
                 out=acc[:], lhsT=key_codes[:, cols].bitcast(FP8X4), lhsT_scale=key_scales[:, cols],
@@ -137,64 +142,52 @@ def tile_picked_kjgclipgmaxfrac_none_p_kernel(
             )
             return acc
 
-        gates = [held([P, S], F32, f"gate{t}") for t in range(PACK)]
-        gated = [held([P, 2, S], F32, f"gated{pair}") for pair in range(2)]
-
-        def gate_rows(t):
-            nc.scalar.copy(b_rows[t][:, :S], score(t, two_codes, two_scales, t)[:])
-            nc.scalar.activation(gates[t][:], b_rows[t][:].indirect(n2_t[:]), ACT.Sigmoid, scale=0.0625)
-
-        def apply_gate(t):
-            nc.vector.tensor_tensor(gated[t // 2][:, t % 2, :], b_rows[t][:, :S], gates[t][:], ALU.mult)
-
-
-        a_banks = [score(t, idx_codes, idx_scales, t) for t in range(PACK)]
-        for t, acc in enumerate(a_banks):
-            if t == 0:
-                nc.scalar.activation(a_rows[t][:, :S], acc[:], ACT.Copy, scale=a_gain[:, t : t + 1])
-            else:
-                nc.vector.tensor_scalar(a_rows[t][:, :S], acc[:], a_gain[:, t : t + 1], None, ALU.mult)
-        w_codes = [held([P, N], U32, f"w_codes{i}") for i in range(2)]
-        w_scales = [held([P, N], U8, f"w_scales{i}") for i in range(2)]
-        quantize(w_codes[0][:], w_scales[0][:], w_grouped[0][:])
-        for side in range(2):
-            interleave(nc.vector.tensor_copy, w_grouped[1][:, side * N // 2 : (side + 1) * N // 2, :], w2_raw[side][:])
-
-        z2_planes = held([P, PACK, S], BF16, "z2_planes")
-        z2_grouped = held([P, S, PACK], BF16, "z2_grouped")
-        z2_codes = held([P, S], U32, "z2_codes")
-        z2_scales = held([P, S], U8, "z2_scales")
+        a_banks = [score(t, idx_codes, idx_scales) for t in range(PACK)]
+        nc.scalar.activation(a_rows[0][:, :S], a_banks[0][:], ACT.Copy, scale=a_gain[:, 0:1])
+        for t in range(1, PACK):
+            nc.vector.tensor_scalar(a_rows[t][:, :S], a_banks[t][:], a_gain[:, t : t + 1], None, ALU.mult)
+        w1_codes, w2_codes = (held([P, N], U32, name) for name in ("w1_codes", "w2_codes"))
+        w1_scales, w2_scales = (held([P, N], U8, name) for name in ("w1_scales", "w2_scales"))
+        w2_left_grouped = held([P, SIDE, PACK], BF16, "w2_left_grouped")
+        interleave(nc.vector.tensor_copy, w1_grouped[:, SIDE:, :], w1_right[:])
+        interleave(nc.vector.tensor_copy, w2_left_grouped[:], w2_left[:])
+        quantize(w1_codes[:], w1_scales[:], w1_grouped[:])
+        quantize(w2_codes[:, :SIDE], w2_scales[:, :SIDE], w2_left_grouped[:])
 
         z_pairs = [held([P, 2, HALF, 2], BF16, f"z_pairs{half}") for half in range(2)]
         z_grouped = [held([P, HALF, PACK], BF16, f"z_grouped{half}") for half in range(2)]
         z_codes = [held([P, HALF], U32, f"z_codes{half}") for half in range(2)]
         z_scales = [held([P, HALF], U8, f"z_scales{half}") for half in range(2)]
+        half_list = HALF * MEMBERS // LIST_ROWS
 
-        def fetch_members(half, pair):
-            members = held([P, 2, HALF * MEMBERS], F32, f"members{half}{pair}")
+        def members_by_twos(step, half, pair):
+            members = held([P, 2, HALF * MEMBERS], F32, f"members{step}")
+            entries = n1_t[:, half_list * half : half_list * (half + 1)]
             for e in range(2):
-                nc.scalar.activation(
-                    members[:, e, :], a_rows[2 * pair + e][:].indirect(n1_t[:, 32 * half : 32 * (half + 1)]), ACT.Copy
-                )
-            return members
-
-        def clip_first(members, tiles, highs, lows):
-            quads = members[:, tiles, :].rearrange("p e (j m) -> p (e j) m", m=MEMBERS)
+                nc.scalar.activation(members[:, e, :], a_rows[2 * pair + e][:].indirect(entries), ACT.Copy)
+            highs = shared.tile([P, 2, HALF, 2], F32, name=f"highs{step}", offset=pair * SIDE_BYTES // 2)
+            lows = shared.tile([P, 2, HALF, 2], F32, name=f"lows{step}", offset=(2 + pair) * SIDE_BYTES // 2)
+            quads = members[:].rearrange("p e (j m) -> p (e j) m", m=MEMBERS)
             for op, dst in ((ALU.max, highs), (ALU.min, lows)):
-                nc.vector.tensor_tensor(dst[:, tiles, :, :].rearrange("p e j m -> p (e j) m"), quads[:, :, 0:2], quads[:, :, 2:4], op)
+                nc.vector.tensor_tensor(dst[:].rearrange("p e j m -> p (e j) m"), quads[:, :, 0:2], quads[:, :, 2:4], op)
+            return highs, lows
 
-        def clip_second(half, pair, tiles, highs, lows, high, low, capped):
+        def cap(half, pair, highs, lows):
+            high = ring.tile([P, 2, HALF], F32, name="high")
+            low = ring.tile([P, 2, HALF], F32, name="low")
+            capped = ring.tile([P, 2, HALF], F32, name="capped")
             for op, dst, src in ((ALU.max, high, highs), (ALU.min, low, lows)):
-                nc.vector.tensor_tensor(dst[:, tiles, :], src[:, tiles, :, 0], src[:, tiles, :, 1], op)
-            for e in range(tiles.start, tiles.stop):
+                nc.vector.tensor_tensor(dst[:], src[:, :, :, 0], src[:, :, :, 1], op)
+            for e in range(2):
                 t = 2 * pair + e
                 if half == 0:
                     own, factor = a_banks[t][:, :HALF], cap_gain[:, t : t + 1]
                 else:
                     own, factor = a_rows[t][:, HALF:S], 1.5
                 nc.vector.scalar_tensor_tensor(capped[:, e, :], own, factor, high[:, e, :], ALU.mult, ALU.min)
+            return capped, low
 
-        def clip_last(half, pair, capped, low):
+        def lift(half, pair, capped, low):
             nc.vector.tensor_tensor(
                 z_pairs[half][:, pair, :, :], capped[:].rearrange("p e j -> p j e"), low[:].rearrange("p e j -> p j e"), ALU.max
             )
@@ -205,41 +198,33 @@ def tile_picked_kjgclipgmaxfrac_none_p_kernel(
                 z_pairs[half][:].rearrange("p w j e -> p (w j e)").bitcast(F32).rearrange("p (w j) -> p j w", w=2),
             )
 
-        units = [(half, pair) for half in range(2) for pair in range(2)]
+        steps = [(half, pair) for half in range(2) for pair in range(2)]
         pending = None
-        for n, (half, pair) in enumerate(units):
-            members = fetch_members(half, pair)
-            highs = shared.tile([P, 2, HALF, 2], F32, name=f"highs{n}", offset=(n % 2) * W_BYTES // 4)
-            lows = shared.tile([P, 2, HALF, 2], F32, name=f"lows{n}", offset=(2 + n % 2) * W_BYTES // 4)
-            high = ring.tile([P, 2, HALF], F32, name="high")
-            low = ring.tile([P, 2, HALF], F32, name="low")
-            capped = ring.tile([P, 2, HALF], F32, name="capped")
-            tiles = slice(0, 2)
-            clip_first(members, tiles, highs, lows)
+        for step, (half, pair) in enumerate(steps):
+            highs, lows = members_by_twos(step, half, pair)
             if pending is not None:
-                clip_last(*pending)
-            clip_second(half, pair, tiles, highs, lows, high, low, capped)
-            pending = (half, pair, capped, low)
-            if n == 0:
-                quantize(w_codes[1][:], w_scales[1][:], w_grouped[1][:])
-            if n == 2:
+                lift(*pending)
+            pending = (half, pair) + cap(half, pair, highs, lows)
+            if (half, pair) == (1, 0):
                 weave(0)
-            if n == 3:
-                quantize(z_codes[0][:], z_scales[0][:], z_grouped[0][:])
-        clip_last(*pending)
+        quantize(z_codes[0][:], z_scales[0][:], z_grouped[0][:])
+        lift(*pending)
 
+        gates = [held([P, S], F32, f"gate{t}") for t in range(PACK)]
+        gated = [held([P, S], F32, f"gated{t}") for t in range(PACK)]
         rival = [held([P, S], F32, f"rival{t}") for t in range(PACK)]
-        larger = [held([P, 2, S], F32, f"larger{pair}") for pair in range(2)]
+        larger = [held([P, S], F32, f"larger{t}") for t in range(PACK)]
+        z2_tiles = held([P, PACK, S], BF16, "z2_tiles")
+        z2_grouped = held([P, S, PACK], BF16, "z2_grouped")
+        z2_codes = held([P, S], U32, "z2_codes")
+        z2_scales = held([P, S], U8, "z2_scales")
 
-        def take_larger(t):
-            nc.scalar.activation(rival[t][:], b_rows[t][:].indirect(n3_t[:]), ACT.Copy)
-            nc.vector.tensor_tensor(larger[t // 2][:, t % 2, :], gated[t // 2][:, t % 2, :], rival[t][:], ALU.max)
-
-        def apply_gain(t):
-            nc.vector.tensor_scalar(z2_planes[:, t, :], larger[t // 2][:, t % 2, :], b_gain[:, t : t + 1], None, ALU.mult)
+        def apply_gate(t):
+            nc.vector.tensor_tensor(gated[t][:], b_rows[t][:, :S], gates[t][:], ALU.mult)
 
         for t in range(PACK):
-            gate_rows(t)
+            nc.scalar.copy(b_rows[t][:, :S], score(t, two_codes, two_scales)[:])
+            nc.scalar.activation(gates[t][:], b_rows[t][:].indirect(n2_t[:]), ACT.Sigmoid, scale=SIXTEENTH)
         apply_gate(0)
         weave(1)
         apply_gate(1)
@@ -248,34 +233,40 @@ def tile_picked_kjgclipgmaxfrac_none_p_kernel(
         apply_gate(3)
         for t in range(PACK + 1):
             if t < PACK:
-                take_larger(t)
+                nc.scalar.activation(rival[t][:], b_rows[t][:].indirect(n3_t[:]), ACT.Copy)
+                nc.vector.tensor_tensor(larger[t][:], gated[t][:], rival[t][:], ALU.max)
             if t > 0:
-                apply_gain(t - 1)
-        interleave(nc.vector.tensor_copy, z2_grouped[:], z2_planes[:])
-        nc.scalar.activation(warm[:, 1:2], rival[PACK - 1][:, 0:1], ACT.Abs_reciprocal_sqrt, bias=0.5, scale=0.0)
+                nc.vector.tensor_scalar(z2_tiles[:, t - 1, :], larger[t - 1][:], b_gain[:, t - 1 : t], None, ALU.mult)
+        interleave(nc.vector.tensor_copy, z2_grouped[:], z2_tiles[:])
+        w2_right_grouped = keep.tile([P, SIDE, PACK], BF16, name="w2_right_grouped", tag=f"gate{PACK - 1}", align_bytes=64)
+        interleave(nc.scalar.copy, w2_right_grouped[:], w2_right[:])
+        nc.scalar.activation(warm[:, 1:2], w2_right_grouped[:, 0, 0:1], ACT.Abs_reciprocal_sqrt, bias=0.5, scale=0.0)
         quantize(z2_codes[:], z2_scales[:], z2_grouped[:])
+        quantize(w2_codes[:, SIDE:], w2_scales[:, SIDE:], w2_right_grouped[:])
 
+        blocks = N // P
         h_rows = b_rows
-        for u in range(N // P):
+        for u in range(blocks):
             acc = psum.tile([P, S], F32, name=f"bank{PACK + u}", tag=f"bank{PACK + u}")
             cols = slice(u * P, (u + 1) * P)
             for half in range(2):
                 nc.tensor.matmul_mx(
-                    out=acc[:, half * HALF : (half + 1) * HALF], lhsT=w_codes[0][:, cols].bitcast(FP8X4),
-                    lhsT_scale=w_scales[0][:, cols], rhs=z_codes[half][:].bitcast(FP8X4),
+                    out=acc[:, half * HALF : (half + 1) * HALF], lhsT=w1_codes[:, cols].bitcast(FP8X4),
+                    lhsT_scale=w1_scales[:, cols], rhs=z_codes[half][:].bitcast(FP8X4),
                     rhs_scale=z_scales[half][:], start=(half == 0), stop=False,
                 )
             nc.tensor.matmul_mx(
-                out=acc[:], lhsT=w_codes[1][:, cols].bitcast(FP8X4), lhsT_scale=w_scales[1][:, cols],
+                out=acc[:], lhsT=w2_codes[:, cols].bitcast(FP8X4), lhsT_scale=w2_scales[:, cols],
                 rhs=z2_codes[:].bitcast(FP8X4), rhs_scale=z2_scales[:], start=False, stop=True,
             )
             nc.vector.tensor_copy(h_rows[u][:, :S], acc[:])
-        names = ("at_n5", "at_n4", "diff", "dist", "numer", "root", "once", "quot")
-        at_n5, at_n4, diff, dist, numer, root, once, quot = (
-            [held([P, S], F32, f"{name}{u}") for u in range(N // P)] for name in names
+
+        names = ("at_n5", "at_n4", "diff", "dist", "numer", "root", "inverse", "quot")
+        at_n5, at_n4, diff, dist, numer, root, inverse, quot = (
+            [held([P, S], F32, f"{name}{u}") for u in range(blocks)] for name in names
         )
 
-        def distance(u):
+        def difference(u):
             nc.scalar.activation(at_n5[u][:], h_rows[u][:].indirect(n5_t[:]), ACT.Copy)
             nc.vector.tensor_tensor(diff[u][:], at_n5[u][:], h_rows[u][:, :S], ALU.subtract)
 
@@ -286,28 +277,27 @@ def tile_picked_kjgclipgmaxfrac_none_p_kernel(
             nc.scalar.activation(at_n4[u][:], h_rows[u][:].indirect(n4_t[:]), ACT.Copy)
             nc.vector.tensor_tensor(numer[u][:], h_rows[u][:, :S], at_n4[u][:], ALU.subtract)
 
-        def divide_once(u):
+        def invert(u):
             nc.scalar.activation(root[u][:], dist[u][:], ACT.Abs_reciprocal_sqrt, bias=0.5)
             if u < SQUARED_ON_SCALAR:
-                nc.scalar.activation(once[u][:], root[u][:], ACT.Square)
+                nc.scalar.activation(inverse[u][:], root[u][:], ACT.Square)
             else:
-                nc.vector.tensor_tensor(once[u][:], root[u][:], root[u][:], ALU.mult)
+                nc.vector.tensor_tensor(inverse[u][:], root[u][:], root[u][:], ALU.mult)
 
-        def divide_twice(u):
-            nc.vector.tensor_tensor(quot[u][:], once[u][:], numer[u][:], ALU.mult)
+        def store(u):
+            nc.vector.tensor_tensor(quot[u][:], inverse[u][:], numer[u][:], ALU.mult)
             nc.sync.dma_start(out[u * P : (u + 1) * P, :], quot[u][:])
 
-        blocks = N // P
-        distance(0)
+        difference(0)
         magnitude(0)
         for u in range(blocks + 1):
             if u + 1 < blocks:
-                distance(u + 1)
+                difference(u + 1)
             if u > 0:
-                divide_twice(u - 1)
+                store(u - 1)
             if u < blocks:
                 numerator(u)
             if u + 1 < blocks:
                 magnitude(u + 1)
             if u < blocks:
-                divide_once(u)
+                invert(u)

@@ -56,7 +56,7 @@ def tile_picked_kjgclipgmaxfrac_none_p_kernel(
             return raw
 
         def interleave(copy, dst, src):
-            copy(dst, src.rearrange("p t c -> p c t"))
+            copy(dst.rearrange("p (g i) t -> p g t i", i=4), src.rearrange("p t (g i) -> p g t i", i=4))
 
         def quantize(codes, scales, grouped):
             nc.vector.quantize_mx(out=codes.bitcast(FP8X4), scales=scales, in_=grouped.rearrange("p c t -> p (c t)"))

from contextlib import ExitStack

import concourse.mybir as mybir

K, T, S, N, G, H = 512, 1024, 256, 512, 2048, 512
FLOPS = 2 * (2 * K * H * S) + 2 * (2 * H * N * S)

F32 = mybir.dt.float32
BF16 = mybir.dt.bfloat16
I32 = mybir.dt.int32
U32 = mybir.dt.uint32
U16 = mybir.dt.uint16
U8 = mybir.dt.uint8
FP8X4 = mybir.dt.float8_e4m3fn_x4
ALU = mybir.AluOpType
ACT = mybir.ActivationFunctionType

P = 128
PACK = 4
QUADRANT = 32
BLOCK_PARTITIONS = 8
LIST_ROWS = 16
MEMBERS = 4
HALF = S // 2
SIDE = N // 2
SIDE_BYTES = PACK * SIDE * 4
SIXTEENTH = 0.0625
A_WINDOW = HALF * MEMBERS + LIST_ROWS
B_WINDOW = 2 * S
SQUARED_ON_SCALAR = 2


def tile_picked_kjgclipgmaxfrac_none_p_kernel(
    tc, x_words, x_scales, d_words, d_scales, gn, gm, w1, w2, offs, k1, two, n1, n2, n3, n4, n5, out
):
    nc = tc.nc
    with ExitStack() as ctx:
        keep = ctx.enter_context(tc.tile_pool(name="keep", bufs=1))
        ring = ctx.enter_context(tc.tile_pool(name="ring", bufs=3))
        shared = ctx.enter_context(tc.tile_pool(name="shared", bufs=1))
        psum = ctx.enter_context(tc.psum_pool(name="psum", bufs=1))

        def held(shape, dtype, name):
            return keep.tile(shape, dtype, name=name, tag=name, align_bytes=64)

        def load_list(name, src):
            tile = keep.tile(list(src.shape), U16, name=name)
            nc.sync.dma_start(tile[:], src)
            return tile

        def as_words(packed):
            return packed[0].rearrange("p n t -> p (n t)").bitcast(I32)

        def load_weights(w, side, raw):
            nc.sync.dma_start(raw[:], w.rearrange("(p t) m -> p t m", t=PACK)[:, :, side * SIDE : (side + 1) * SIDE])
            return raw

        def interleave(copy, dst, src):
            copy(dst.rearrange("p (g i) t -> p g t i", i=4), src.rearrange("p t (g i) -> p g t i", i=4))

        def quantize(codes, scales, grouped):
            nc.vector.quantize_mx(out=codes.bitcast(FP8X4), scales=scales, in_=grouped.rearrange("p c t -> p (c t)"))

        d_bytes = held([P, G], U8, "d_bytes")
        x_bytes = held([P, T], U8, "x_bytes")
        nc.vector.memset(d_bytes[:].bitcast(I32), 0)
        nc.gpsimd.memset(x_bytes[:].bitcast(I32), 0)
        w1_left = load_weights(w1, 0, held([P, PACK, SIDE], F32, "w1_left"))
        k1_t = load_list("k1_t", k1)
        nc.sync.dma_start(d_bytes[0:P:BLOCK_PARTITIONS, :].bitcast(I32), d_scales[0].bitcast(I32))
        nc.sync.dma_start(x_bytes[0:P:BLOCK_PARTITIONS, :].bitcast(I32), x_scales[0].bitcast(I32))
        offs_t = load_list("offs_t", offs)
        two_t = load_list("two_t", two)
        d_table = shared.tile([P, G], I32, name="d_table", offset=0)
        nc.sync.dma_start(d_table[:], as_words(d_words))
        x_table = shared.tile([P, T], I32, name="x_table", offset=2 * SIDE_BYTES)
        nc.sync.dma_start(x_table[:], as_words(x_words))
        gn_t = held([P, PACK], F32, "gn_t")
        gm_t = held([P, PACK], F32, "gm_t")
        nc.sync.dma_start(gn_t[:], gn.rearrange("(p t) o -> p (t o)", t=PACK))
        nc.sync.dma_start(gm_t[:], gm.rearrange("(p t) o -> p (t o)", t=PACK))
        n1_t = load_list("n1_t", n1)
        n2_t = load_list("n2_t", n2)
        n3_t = load_list("n3_t", n3)
        n5_t = load_list("n5_t", n5)
        n4_t = load_list("n4_t", n4)

        a_rows = [held([P, A_WINDOW], F32, f"a_rows{t}") for t in range(PACK)]
        b_rows = [held([P, B_WINDOW], F32, f"b_rows{t}") for t in range(PACK)]
        for tile in b_rows + a_rows:
            nc.vector.memset(tile[:, S:], 0.0)
        warm = held([P, 2], F32, "warm")
        nc.scalar.activation(warm[:, 0:1], b_rows[0][:, S : S + 1], ACT.Sigmoid)
        scale_rows = held([P, H + 2 * S], U8, "scale_rows")
        nc.vector.memset(scale_rows[:].bitcast(I32), 0)
        a_gain = held([P, PACK], F32, "a_gain")
        b_gain = held([P, PACK], F32, "b_gain")
        cap_gain = held([P, PACK], F32, "cap_gain")
        nc.gpsimd.tensor_scalar(cap_gain[:], gn_t[:], 1.5 * SIXTEENTH, 0.0, ALU.mult, ALU.add)
        nc.gpsimd.tensor_scalar(a_gain[:], gn_t[:], SIXTEENTH, 0.0, ALU.mult, ALU.add)
        nc.gpsimd.tensor_scalar(b_gain[:], gm_t[:], SIXTEENTH, 0.0, ALU.mult, ALU.add)

        picked_bytes = held([P, H + 2 * S], U8, "picked_bytes")
        nc.vector.tensor_copy(picked_bytes[:, :H], d_bytes[:].indirect(k1_t[:]))
        nc.vector.tensor_copy(picked_bytes[:, H : H + S], x_bytes[:].indirect(two_t[:]))
        nc.vector.tensor_copy(picked_bytes[:, H + S :], x_bytes[:].indirect(offs_t[:]))
        for s in range(QUADRANT // BLOCK_PARTITIONS):
            nc.scalar.dma_start(
                scale_rows[s:P:QUADRANT, :].bitcast(I32), picked_bytes[BLOCK_PARTITIONS * s : P : QUADRANT, :].bitcast(I32)
            )
        two_scales, idx_scales = scale_rows[:, H : H + S], scale_rows[:, H + S :]

        key_words = held([P, H], U32, "key_words")
        nc.vector.tensor_copy(key_words[:], d_table[:].bitcast(U32).indirect(k1_t[:]))
        key_codes = held([P, H], I32, "key_codes")
        nc.vector.tensor_copy(
            key_codes[:].rearrange("p (t c i) -> p c t i", t=PACK, i=4),
            key_words[:].bitcast(I32).rearrange("p (c i t) -> p c t i", t=PACK, i=4),
        )
        key_scales = held([P, H], U8, "key_scales")
        nc.vector.tensor_copy(
            key_scales[:].rearrange("p (t m) -> p t m", t=PACK), scale_rows[:, :H].rearrange("p (m t) -> p t m", t=PACK)
        )
        idx_codes = held([P, S], U32, "idx_codes")
        nc.vector.tensor_copy(idx_codes[:], x_table[:].bitcast(U32).indirect(offs_t[:]))
        two_codes = held([P, S], U32, "two_codes")
        nc.vector.tensor_copy(two_codes[:], x_table[:].bitcast(U32).indirect(two_t[:]))

        w1_right, w2_left, w2_right = (
            load_weights(w, side, shared.tile([P, PACK, SIDE], F32, name=f"w_raw{n}", offset=n * SIDE_BYTES))
            for n, (w, side) in enumerate(((w1, 1), (w2, 0), (w2, 1)))
        )
        w1_grouped = held([P, N, PACK], BF16, "w1_grouped")
        interleave(nc.scalar.copy, w1_grouped[:, :SIDE, :], w1_left[:])

        def score(t, codes, scales):
            acc = psum.tile([P, S], F32, name=f"bank{t}", tag=f"bank{t}")
            cols = slice(t * P, (t + 1) * P)
            nc.tensor.matmul_mx(
                out=acc[:], lhsT=key_codes[:, cols].bitcast(FP8X4), lhsT_scale=key_scales[:, cols],
                rhs=codes[:].bitcast(FP8X4), rhs_scale=scales, start=True, stop=True,
            )
            return acc

        a_banks = [score(t, idx_codes, idx_scales) for t in range(PACK)]
        nc.scalar.activation(a_rows[0][:, :S], a_banks[0][:], ACT.Copy, scale=a_gain[:, 0:1])
        for t in range(1, PACK):
            nc.vector.tensor_scalar(a_rows[t][:, :S], a_banks[t][:], a_gain[:, t : t + 1], None, ALU.mult)
        w1_codes, w2_codes = (held([P, N], U32, name) for name in ("w1_codes", "w2_codes"))
        w1_scales, w2_scales = (held([P, N], U8, name) for name in ("w1_scales", "w2_scales"))
        w2_left_grouped = held([P, SIDE, PACK], BF16, "w2_left_grouped")
        interleave(nc.vector.tensor_copy, w1_grouped[:, SIDE:, :], w1_right[:])
        interleave(nc.vector.tensor_copy, w2_left_grouped[:], w2_left[:])
        quantize(w1_codes[:], w1_scales[:], w1_grouped[:])
        quantize(w2_codes[:, :SIDE], w2_scales[:, :SIDE], w2_left_grouped[:])

        z_pairs = [held([P, 2, HALF, 2], BF16, f"z_pairs{half}") for half in range(2)]
        z_grouped = [held([P, HALF, PACK], BF16, f"z_grouped{half}") for half in range(2)]
        z_codes = [held([P, HALF], U32, f"z_codes{half}") for half in range(2)]
        z_scales = [held([P, HALF], U8, f"z_scales{half}") for half in range(2)]
        half_list = HALF * MEMBERS // LIST_ROWS

        def members_by_twos(step, half, pair):
            members = held([P, 2, HALF * MEMBERS], F32, f"members{step}")
            entries = n1_t[:, half_list * half : half_list * (half + 1)]
            for e in range(2):
                nc.scalar.activation(members[:, e, :], a_rows[2 * pair + e][:].indirect(entries), ACT.Copy)
            highs = shared.tile([P, 2, HALF, 2], F32, name=f"highs{step}", offset=pair * SIDE_BYTES // 2)
            lows = shared.tile([P, 2, HALF, 2], F32, name=f"lows{step}", offset=(2 + pair) * SIDE_BYTES // 2)
            quads = members[:].rearrange("p e (j m) -> p (e j) m", m=MEMBERS)
            for op, dst in ((ALU.max, highs), (ALU.min, lows)):
                nc.vector.tensor_tensor(dst[:].rearrange("p e j m -> p (e j) m"), quads[:, :, 0:2], quads[:, :, 2:4], op)
            return highs, lows

        def cap(half, pair, highs, lows):
            high = ring.tile([P, 2, HALF], F32, name="high")
            low = ring.tile([P, 2, HALF], F32, name="low")
            capped = ring.tile([P, 2, HALF], F32, name="capped")
            for op, dst, src in ((ALU.max, high, highs), (ALU.min, low, lows)):
                nc.vector.tensor_tensor(dst[:], src[:, :, :, 0], src[:, :, :, 1], op)
            for e in range(2):
                t = 2 * pair + e
                if half == 0:
                    own, factor = a_banks[t][:, :HALF], cap_gain[:, t : t + 1]
                else:
                    own, factor = a_rows[t][:, HALF:S], 1.5
                nc.vector.scalar_tensor_tensor(capped[:, e, :], own, factor, high[:, e, :], ALU.mult, ALU.min)
            return capped, low

        def lift(half, pair, capped, low):
            nc.vector.tensor_tensor(
                z_pairs[half][:, pair, :, :], capped[:].rearrange("p e j -> p j e"), low[:].rearrange("p e j -> p j e"), ALU.max
            )

        def weave(half):
            nc.vector.tensor_copy(
                z_grouped[half][:].rearrange("p j t -> p (j t)").bitcast(F32).rearrange("p (j w) -> p j w", w=2),
                z_pairs[half][:].rearrange("p w j e -> p (w j e)").bitcast(F32).rearrange("p (w j) -> p j w", w=2),
            )

        steps = [(half, pair) for half in range(2) for pair in range(2)]
        pending = None
        for step, (half, pair) in enumerate(steps):
            highs, lows = members_by_twos(step, half, pair)
            if pending is not None:
                lift(*pending)
            pending = (half, pair) + cap(half, pair, highs, lows)
            if (half, pair) == (1, 0):
                weave(0)
        quantize(z_codes[0][:], z_scales[0][:], z_grouped[0][:])
        lift(*pending)

        gates = [held([P, S], F32, f"gate{t}") for t in range(PACK)]
        gated = [held([P, S], F32, f"gated{t}") for t in range(PACK)]
        rival = [held([P, S], F32, f"rival{t}") for t in range(PACK)]
        larger = [held([P, S], F32, f"larger{t}") for t in range(PACK)]
        z2_tiles = held([P, PACK, S], BF16, "z2_tiles")
        z2_grouped = held([P, S, PACK], BF16, "z2_grouped")
        z2_codes = held([P, S], U32, "z2_codes")
        z2_scales = held([P, S], U8, "z2_scales")

        def apply_gate(t):
            nc.vector.tensor_tensor(gated[t][:], b_rows[t][:, :S], gates[t][:], ALU.mult)

        for t in range(PACK):
            nc.scalar.copy(b_rows[t][:, :S], score(t, two_codes, two_scales)[:])
            nc.scalar.activation(gates[t][:], b_rows[t][:].indirect(n2_t[:]), ACT.Sigmoid, scale=SIXTEENTH)
        apply_gate(0)
        weave(1)
        apply_gate(1)
        apply_gate(2)
        quantize(z_codes[1][:], z_scales[1][:], z_grouped[1][:])
        apply_gate(3)
        for t in range(PACK + 1):
            if t < PACK:
                nc.scalar.activation(rival[t][:], b_rows[t][:].indirect(n3_t[:]), ACT.Copy)
                nc.vector.tensor_tensor(larger[t][:], gated[t][:], rival[t][:], ALU.max)
            if t > 0:
                nc.vector.tensor_scalar(z2_tiles[:, t - 1, :], larger[t - 1][:], b_gain[:, t - 1 : t], None, ALU.mult)
        interleave(nc.vector.tensor_copy, z2_grouped[:], z2_tiles[:])
        w2_right_grouped = keep.tile([P, SIDE, PACK], BF16, name="w2_right_grouped", tag=f"gate{PACK - 1}", align_bytes=64)
        interleave(nc.scalar.copy, w2_right_grouped[:], w2_right[:])
        nc.scalar.activation(warm[:, 1:2], w2_right_grouped[:, 0, 0:1], ACT.Abs_reciprocal_sqrt, bias=0.5, scale=0.0)
        quantize(z2_codes[:], z2_scales[:], z2_grouped[:])
        quantize(w2_codes[:, SIDE:], w2_scales[:, SIDE:], w2_right_grouped[:])

        blocks = N // P
        h_rows = b_rows
        for u in range(blocks):
            acc = psum.tile([P, S], F32, name=f"bank{PACK + u}", tag=f"bank{PACK + u}")
            cols = slice(u * P, (u + 1) * P)
            for half in range(2):
                nc.tensor.matmul_mx(
                    out=acc[:, half * HALF : (half + 1) * HALF], lhsT=w1_codes[:, cols].bitcast(FP8X4),
                    lhsT_scale=w1_scales[:, cols], rhs=z_codes[half][:].bitcast(FP8X4),
                    rhs_scale=z_scales[half][:], start=(half == 0), stop=False,
                )
            nc.tensor.matmul_mx(
                out=acc[:], lhsT=w2_codes[:, cols].bitcast(FP8X4), lhsT_scale=w2_scales[:, cols],
                rhs=z2_codes[:].bitcast(FP8X4), rhs_scale=z2_scales[:], start=False, stop=True,
            )
            nc.vector.tensor_copy(h_rows[u][:, :S], acc[:])

        names = ("at_n5", "at_n4", "diff", "dist", "numer", "root", "inverse", "quot")
        at_n5, at_n4, diff, dist, numer, root, inverse, quot = (
            [held([P, S], F32, f"{name}{u}") for u in range(blocks)] for name in names
        )

        def difference(u):
            nc.scalar.activation(at_n5[u][:], h_rows[u][:].indirect(n5_t[:]), ACT.Copy)
            nc.vector.tensor_tensor(diff[u][:], at_n5[u][:], h_rows[u][:, :S], ALU.subtract)

        def magnitude(u):
            nc.vector.scalar_tensor_tensor(dist[u][:], diff[u][:], -1.0, diff[u][:], ALU.mult, ALU.max)

        def numerator(u):
            nc.scalar.activation(at_n4[u][:], h_rows[u][:].indirect(n4_t[:]), ACT.Copy)
            nc.vector.tensor_tensor(numer[u][:], h_rows[u][:, :S], at_n4[u][:], ALU.subtract)

        def invert(u):
            nc.scalar.activation(root[u][:], dist[u][:], ACT.Abs_reciprocal_sqrt, bias=0.5)
            if u < SQUARED_ON_SCALAR:
                nc.scalar.activation(inverse[u][:], root[u][:], ACT.Square)
            else:
                nc.vector.tensor_tensor(inverse[u][:], root[u][:], root[u][:], ALU.mult)

        def store(u):
            nc.vector.tensor_tensor(quot[u][:], inverse[u][:], numer[u][:], ALU.mult)
            nc.sync.dma_start(out[u * P : (u + 1) * P, :], quot[u][:])

        difference(0)
        magnitude(0)
        for u in range(blocks + 1):
            if u + 1 < blocks:
                difference(u + 1)
            if u > 0:
                store(u - 1)
            if u < blocks:
                numerator(u)
            if u + 1 < blocks:
                magnitude(u + 1)
            if u < blocks:
                invert(u)
